import numpy as np
import ml_dtypes


def mxq(x, axis, fmt="e4m3"):
    dtype, down = {"e4m3": (ml_dtypes.float8_e4m3fn, 7), "e5m2": (ml_dtypes.float8_e5m2, 14)}[fmt]
    v = np.moveaxis(np.asarray(x, np.float32).astype(ml_dtypes.bfloat16).astype(np.float64), axis, -1)
    blocks = v.reshape(v.shape[:-1] + (-1, 32))
    amax = np.abs(blocks).max(-1, keepdims=True)
    byte = np.maximum(np.where(amax > 0, np.frexp(amax)[1] - 1 + 127, 0) - down, 1)
    scale = np.exp2(byte - 127.0)
    codes = (blocks / scale).astype(np.float32).astype(dtype).astype(np.float64)
    return np.moveaxis((codes * scale).reshape(v.shape), -1, axis)


WIDE = False


def mx_kscale(k):
    if not WIDE:
        return np.ones(k)
    levels = np.array([10, -10, 5, -5, 0])
    if k % 512:
        return np.exp2(np.random.permutation(np.resize(levels, k // 32))).repeat(32)
    a = np.empty((k // 512, 16))
    for p in range(k // 512):
        a[p, :8] = np.random.permutation(np.resize(levels, 8))
        for g in range(8):
            far = levels[np.abs(levels - a[p, g]) >= 10]
            a[p, g + 8] = far[np.random.randint(len(far))]
    return np.exp2(a.ravel()).repeat(32)


BF16 = ml_dtypes.bfloat16


def bf(x):
    return np.asarray(x, np.float32).astype(BF16)


def f64(x):
    return np.asarray(x).astype(np.float64)


E2M1 = np.array([0.0, 0.5, 1.0, 1.5, 2.0, 3.0, 4.0, 6.0, -0.0, -0.5, -1.0, -1.5, -2.0, -3.0, -4.0, -6.0])


def pack_weight(w, fmt):
    k, n = w.shape
    w = f64(bf(w)).reshape(k // 32, 32, n)
    amax = np.abs(w).max(1)
    if fmt == "e4m3":
        byte = np.frexp(amax)[1] - 1 + 127 - 7
    else:
        mant, ex = np.frexp(amax / 6.0)
        byte = np.where(mant > 0.5, ex, ex - 1) + 127
    byte = np.clip(np.where(amax > 0, byte, 1), 1, 254)
    scaled = (w * np.exp2(127.0 - byte)[:, None, :]).reshape(k, n).astype(np.float32)
    by_word = np.ascontiguousarray(scaled.reshape(k // 512, 128, 4, n).transpose(0, 1, 3, 2))
    if fmt == "e4m3":
        words = by_word.astype(ml_dtypes.float8_e4m3fn).view(np.uint8)
    else:
        c = by_word.astype(ml_dtypes.float4_e2m1fn).view(np.uint8) & 0xF
        words = c[..., 0::2] | (c[..., 1::2] << 4)
    return np.ascontiguousarray(words), np.ascontiguousarray(byte.astype(np.uint8).reshape(k // 512, 16, n))


def unpack_weight(words, scales, fmt):
    g, p, n, _ = words.shape
    if fmt == "e4m3":
        vals = np.ascontiguousarray(words).view(ml_dtypes.float8_e4m3fn).astype(np.float64)
    else:
        nib = np.empty((g, p, n, 4), np.uint8)
        nib[..., 0::2] = words & 0xF
        nib[..., 1::2] = words >> 4
        vals = E2M1[nib]
    vals = vals * np.repeat(np.exp2(scales.astype(np.float64) - 127.0), 8, axis=1)[..., None]
    return vals.transpose(0, 1, 3, 2).reshape(g * 512, n)
def pack4(w):
    words, scales = pack_weight(w, "e2m1")
    return words.reshape(words.shape[0], 128, -1), scales


def unpack4(words, scales):
    return unpack_weight(words.reshape(words.shape[0], 128, -1, 2), scales, "e2m1")


def planes(Y):
    n, m = Y.shape
    b = f64(bf(Y)).reshape(n // 32, 32, m)
    amax = np.abs(b).max(1)
    byte = np.clip(np.where(amax > 0, np.frexp(amax)[1] - 1 + 127 - 7, 1), 1, 254)
    codes = (b * np.exp2(127.0 - byte)[:, None, :]).reshape(n, m).astype(np.float32).astype(ml_dtypes.float8_e4m3fn).view(np.uint8)
    words = codes.reshape(n // 512, 128, 4, m).transpose(0, 1, 3, 2)
    return np.ascontiguousarray(words), np.ascontiguousarray(byte.astype(np.uint8).reshape(n // 512, 16, m))


N, O, F = 1024, 512, 1024


def silu_slope(a):
    s = 1.0 / (1.0 + np.exp(-a))
    return s * (1.0 + a * (1.0 - s))


def setup_inputs():
    s1, s2 = mx_kscale(O), mx_kscale(O)
    t = mx_kscale(N)
    amp = N**0.25
    dy1 = bf(np.random.standard_normal((N, O)) * amp * s1[None, :] * t[:, None])
    w1_words, w1_scales = pack4((np.random.standard_normal((F, O)) / np.sqrt(O) / s1[None, :]).T)
    dy2 = bf(np.random.standard_normal((N, O)) * amp * s2[None, :] / t[:, None])
    w2_words, w2_scales = pack4((np.random.standard_normal((F, O)) / np.sqrt(O) / s2[None, :]).T)
    return {
        "dy1": dy1,
        "w1_words": w1_words,
        "w1_scales": w1_scales,
        "dy2": dy2,
        "w2_words": w2_words,
        "w2_scales": w2_scales,
        "a": bf(np.random.standard_normal((N, F))),
        "g_old": bf(0.3 * np.random.standard_normal((F, F))),
    }


def core(dy1, w1_words, w1_scales, dy2, w2_words, w2_scales, a, g_old):
    a = f64(a)
    n = a.shape[0]
    m = silu_slope(a)
    d1 = (mxq(f64(dy1), 1, "e4m3") @ unpack4(w1_words, w1_scales)) * m
    d2 = (mxq(f64(dy2), 1, "e4m3") @ unpack4(w2_words, w2_scales)) * m
    c = (mxq(d1, 0, "e4m3").T @ mxq(d2, 0, "e4m3")) / n
    return 0.5 * f64(g_old) + 0.5 * c


def reference(dy1, w1_words, w1_scales, dy2, w2_words, w2_scales, a, g_old):
    R_out = core(dy1, w1_words, w1_scales, dy2, w2_words, w2_scales, a, g_old)
    words, scales = planes(R_out.T)
    return R_out, words, scales

@@ -1,0 +1,365 @@
+from contextlib import ExitStack
+
+import concourse.mybir as mybir
+from concourse.masks import make_identity
+
+F32 = mybir.dt.float32
+BF16 = mybir.dt.bfloat16
+U32 = mybir.dt.uint32
+I32 = mybir.dt.int32
+U8 = mybir.dt.uint8
+FP8X4 = mybir.dt.float8_e4m3fn_x4
+FP4X4 = mybir.dt.float4_e2m1fn_x4
+ACT = mybir.ActivationFunctionType
+ALU = mybir.AluOpType
+
+N, O, F = 1024, 512, 1024
+P = 128
+FLOPS = 2 * 2 * N * O * F + 2 * N * F * F
+NB = F // P
+
+
+def tile_twotaskkroneckergradientcrossfactorema_x2_kernel(
+    tc, dy1, w1_words, w1_scales, dy2, w2_words, w2_scales, a, g_old, out_0, out_1, out_2
+):
+    nc = tc.nc
+    dy_in = {1: dy1, 2: dy2}
+    w_in = {1: (w1_words, w1_scales), 2: (w2_words, w2_scales)}
+    d_scale = {1: -1.0 / 2048.0, 2: -1.0}
+
+    with ExitStack() as ctx:
+        keep = ctx.enter_context(tc.tile_pool(name="keep", bufs=1))
+        work = ctx.enter_context(tc.tile_pool(name="work", bufs=3))
+        psum = ctx.enter_context(tc.psum_pool(name="psum", bufs=2))
+
+        ident = keep.tile([P, P], F32, name="ident")
+        make_identity(nc, ident[:])
+        warm = keep.tile([P, 2], F32, name="warm")
+
+        ctx.enter_context(tc.manual_schedule())
+
+        dyr, dyc, dys, ww, ws = {}, {}, {}, {}, {}
+        for t in (1, 2):
+            ww[t] = keep.tile([P, 2 * F], U8, name="ww%d" % t, align_bytes=64)
+            ws[t] = keep.tile([P, F], U8, name="ws%d" % t, align_bytes=64)
+            for g in (0, 1):
+                dyr[t, g] = keep.tile([P, 4, O], BF16, name="dyr%d%d" % (t, g), align_bytes=64)
+                dyc[t, g] = keep.tile([P, 512], U32, name="dyc%d%d" % (t, g), align_bytes=64)
+                dys[t, g] = keep.tile([P, 512], U8, name="dys%d%d" % (t, g), align_bytes=64)
+        chunks = [(0, 0), (1, 0), (0, 1), (1, 1)]
+        at, st, rt = {}, {}, {}
+        for c in chunks:
+            at[c] = keep.tile([P, 4, 512], BF16, name="a%d%d" % c, align_bytes=64)
+            st[c] = keep.tile([P, 2048], F32, name="s%d%d" % c, align_bytes=64)
+            rt[c] = keep.tile([P, 2048], F32, name="r%d%d" % c, align_bytes=64)
+        gt = {}
+        for b in (0, 1):
+            gt[b] = keep.tile([P, 4, F], BF16, name="gt%d" % b, align_bytes=64)
+        d2c, d2s = {}, {}
+        for g in (0, 1):
+            d2c[g] = keep.tile([P, F], U32, name="d2c%d" % g, align_bytes=64)
+            d2s[g] = keep.tile([P, F], U8, name="d2s%d" % g, align_bytes=64)
+        pscale = keep.tile([P, 2, F], U8, name="pscale", align_bytes=64)
+
+        nc.vector.memset(ws[2][:].bitcast(I32), 0)
+        nc.vector.memset(warm[:], 0.0)
+        nc.vector.memset(ws[1][:].bitcast(I32), 0)
+
+        def load_dy(t, g, parts=1):
+            v = dy_in[t].rearrange("(g p t) o -> g p t o", p=P, t=4)
+            n = 4 // parts
+            for k in range(0, 4, n):
+                nc.sync.dma_start(out=dyr[t, g][:, k : k + n, :], in_=v[g, :, k : k + n, :])
+
+        def load_a(c):
+            g, h = c
+            v = a.rearrange("(g p t) f -> g p t f", p=P, t=4)
+            nc.sync.dma_start(out=at[c][:], in_=v[g, :, :, 512 * h : 512 * (h + 1)])
+
+        def load_w(t):
+            nc.sync.dma_start(out=ww[t][:].bitcast(I32), in_=w_in[t][0][0].bitcast(I32))
+
+        def load_ws(t, eng):
+            for q in range(4):
+                eng.dma_start(
+                    out=ws[t][32 * q : 32 * q + 4, :].bitcast(I32),
+                    in_=w_in[t][1][0, 4 * q : 4 * q + 4, :].bitcast(I32),
+                )
+
+        load_dy(2, 0, 2)
+        load_a(chunks[0])
+        load_ws(2, nc.scalar)
+        load_ws(1, nc.gpsimd)
+        load_dy(2, 1)
+        load_a(chunks[1])
+        load_dy(1, 0)
+        load_dy(1, 1)
+        load_w(2)
+        load_w(1)
+        load_a(chunks[2])
+        load_a(chunks[3])
+        gv = g_old.rearrange("(b i p) f -> b p i f", p=P, i=4)
+        for b in (0, 1):
+            nc.sync.dma_start(out=gt[b][:], in_=gv[b])
+
+        def act(c, pair, dst, func, scale):
+            src = at[c][:, :, 256 * pair : 256 * (pair + 1)].rearrange("p t f -> p f t")
+            o = dst[c][:, 1024 * pair : 1024 * (pair + 1)].rearrange("p (f t) -> p f t", t=4)
+            nc.scalar.activation(out=o, in_=src, func=func, scale=scale)
+
+        nc.scalar.activation(out=warm[:, 1:2], in_=warm[:, 0:1], func=ACT.Silu)
+        for c in chunks[:2]:
+            for pair in (0, 1):
+                act(c, pair, rt, ACT.Silu, -1.0)
+        for c in chunks:
+            for pair in (0, 1):
+                act(c, pair, st, ACT.Sigmoid, 1.0)
+        def silu_pair(p):
+            act(chunks[p // 2], p % 2, rt, ACT.Silu, -1.0)
+
+        silu_pair(4)
+
+        def slope(c, pair):
+            sl = slice(1024 * pair, 1024 * (pair + 1))
+            nc.vector.scalar_tensor_tensor(
+                out=rt[c][:, sl], in0=rt[c][:, sl], scalar=1.0, in1=st[c][:, sl],
+                op0=ALU.subtract, op1=ALU.mult,
+            )
+
+        def dy_bank(t, g, b):
+            bank = psum.tile([P, 2, 2, P], F32, name="tp", bufs=2)
+            for k in (0, 1):
+                words = dyr[t, g][:, 2 * b + k, :].bitcast(F32)
+                for u in (0, 1):
+                    nc.tensor.transpose(bank[:, k, u, :], words[:, u:256:2], ident[:])
+            grouped = work.tile([P, 1024], BF16, name="dyg", align_bytes=64, bufs=4)
+            nc.vector.tensor_copy(
+                out=grouped[:].bitcast(F32).rearrange("p (t r u) -> p t r u", t=2, u=2),
+                in_=bank[:].rearrange("p t u r -> p t r u"),
+            )
+            return grouped
+
+        def dy_quant(t, g, b, grouped):
+            nc.vector.quantize_mx(
+                out=dyc[t, g][:, 256 * b : 256 * (b + 1)].bitcast(FP8X4),
+                scales=dys[t, g][:, 256 * b : 256 * (b + 1)],
+                in_=grouped[:],
+            )
+
+        def dy_prep(t):
+            prev = None
+            for g in (0, 1):
+                for b in (0, 1):
+                    cur = (t, g, b, dy_bank(t, g, b))
+                    if prev:
+                        dy_quant(*prev)
+                    prev = cur
+            dy_quant(*prev)
+
+        units = [(2, c[0], 4 * c[1] + j) for c in chunks for j in range(4)]
+        units += [(1, g, i) for i in range(NB) for g in (0, 1)]
+        banks = {}
+
+        def mm1(k):
+            if k >= len(units):
+                return
+            t, g, fb = units[k]
+            bank = psum.tile([P, 4, P], F32, name="s1", bufs=4)
+            for q in range(4):
+                nc.tensor.matmul_mx(
+                    out=bank[:, q, :],
+                    lhsT=dyc[t, g][:, P * q : P * (q + 1)].bitcast(FP8X4),
+                    lhsT_scale=dys[t, g][:, P * q : P * (q + 1)],
+                    rhs=ww[t][:, 256 * fb : 256 * (fb + 1)].bitcast(FP4X4),
+                    rhs_scale=ws[t][:, P * fb : P * (fb + 1)],
+                    start=True,
+                    stop=True,
+                )
+            banks[k] = bank
+
+        def d_mul(k, out):
+            t, g, fb = units[k]
+            nm = rt[g, fb // 4][:, 512 * (fb % 4) : 512 * (fb % 4 + 1)]
+            nc.vector.scalar_tensor_tensor(
+                out=out.rearrange("p (f t) -> p f t", t=4),
+                in0=nm.rearrange("p (f t) -> p f t", t=4),
+                scalar=d_scale[t],
+                in1=banks[k][:].rearrange("p t f -> p f t"),
+                op0=ALU.mult,
+                op1=ALU.mult,
+            )
+
+        def d_mul_pool(k, out):
+            t, g, fb = units[k]
+            nm = rt[g, fb // 4][:, 512 * (fb % 4) : 512 * (fb % 4 + 1)]
+            tmp = work.tile([P, 512], F32, name="tmp", align_bytes=64)
+            nc.scalar.activation(
+                out=tmp[:].rearrange("p (f t) -> p f t", t=4),
+                in_=banks[k][:].rearrange("p t f -> p f t"),
+                func=ACT.Copy,
+                scale=d_scale[t],
+            )
+            nc.gpsimd.tensor_tensor(out=out, in0=tmp[:], in1=nm, op=ALU.mult)
+
+        dy_prep(2)
+        dy_prep(1)
+        for k in range(4):
+            mm1(k)
+
+        def d2_quant(j, dg):
+            t, g, fb = units[2 * j]
+            sl = slice(P * fb, P * (fb + 2))
+            nc.vector.quantize_mx(
+                out=d2c[g][:, sl].bitcast(FP8X4),
+                scales=d2s[g][:, sl],
+                in_=dg[:].rearrange("p a b -> p (a b)"),
+            )
+
+        slope(chunks[0], 0)
+        prev = None
+        for j in range(8):
+            dg = work.tile([P, 2, 512], BF16, name="dg", align_bytes=64, bufs=4)
+            for e in (0, 1):
+                k = 2 * j + e
+                if e == 0 and j >= 2:
+                    d_mul_pool(k, dg[:, e, :])
+                else:
+                    d_mul(k, dg[:, e, :])
+                mm1(k + 4)
+            if 2 <= j < 5:
+                silu_pair(j + 3)
+            if j < 7:
+                slope(chunks[(j + 1) // 2], (j + 1) % 2)
+            if prev:
+                d2_quant(*prev)
+            prev = (j, dg)
+        cb, rr, rb, pg, tb, d1 = {}, {}, {}, {}, {}, {}
+        o0 = out_0.rearrange("(b p) f -> b p f", p=P)
+        o1 = out_1.bitcast(I32).rearrange("g p m o -> p g (m o)")
+        o2 = out_2.bitcast(I32).rearrange("g r m -> r g m")
+
+        def d1_mul(i):
+            dg = work.tile([P, 2, 512], BF16, name="dg", align_bytes=64, bufs=4)
+            for g in (0, 1):
+                k = 16 + 2 * i + g
+                if g == 0:
+                    d_mul_pool(k, dg[:, g, :])
+                else:
+                    d_mul(k, dg[:, g, :])
+                mm1(k + 4)
+            return dg
+
+        def d1_quant(i, dg):
+            codes = work.tile([P, 2, P], U32, name="d1c", align_bytes=64)
+            scales = work.tile([P, 2, P], U8, name="d1s", align_bytes=64)
+            nc.vector.quantize_mx(
+                out=codes[:].rearrange("p a b -> p (a b)").bitcast(FP8X4),
+                scales=scales[:].rearrange("p a b -> p (a b)"),
+                in_=dg[:].rearrange("p a b -> p (a b)"),
+            )
+            d1[i] = (codes, scales)
+
+        def c_mm(i):
+            codes, scales = d1[i]
+            for h in (0, 1):
+                bank = psum.tile([P, 512], F32, name="cb", bufs=2)
+                for g in (0, 1):
+                    nc.tensor.matmul_mx(
+                        out=bank[:],
+                        lhsT=codes[:, g, :].bitcast(FP8X4),
+                        lhsT_scale=scales[:, g, :],
+                        rhs=d2c[g][:, 512 * h : 512 * (h + 1)].bitcast(FP8X4),
+                        rhs_scale=d2s[g][:, 512 * h : 512 * (h + 1)],
+                        start=(g == 0),
+                        stop=(g == 1),
+                    )
+                cb[i, h] = bank
+
+        def blend(i):
+            res = work.tile([P, F], F32, name="res", align_bytes=64)
+            for h in (0, 1):
+                sl = slice(512 * h, 512 * (h + 1))
+                nc.vector.scalar_tensor_tensor(
+                    out=res[:, sl], in0=gt[i // 4][:, i % 4, sl], scalar=0.5, in1=cb[i, h][:],
+                    op0=ALU.mult, op1=ALU.add,
+                )
+            nc.sync.dma_start(out=o0[i], in_=res[:])
+            rr[i] = res
+
+        def cast(i):
+            b16 = work.tile([P, 2, 512], BF16, name="b16", align_bytes=64)
+            rb[i] = b16
+            for h in (0, 1):
+                o = b16[:, h, :].rearrange("q (u p e) -> q u p e", u=2, e=2)
+                src = rr[i][:, 512 * h : 512 * (h + 1)].rearrange("q (p u e) -> q u p e", u=2, e=2)
+                if i == NB - 1 and h == 1:
+                    nc.vector.tensor_copy(out=o, in_=src)
+                else:
+                    nc.scalar.activation(out=o, in_=src, func=ACT.Copy)
+
+        def turn(i):
+            last = i == NB - 1
+            words = rb[i][:].rearrange("q h x -> q (h x)").bitcast(F32)
+            tb[i] = []
+            for k in range(4):
+                if k == 0 or (last and k == 2):
+                    bank = psum.tile([P, 4, P], F32, name="tp", bufs=2)
+                    tb[i].append(bank)
+                nc.tensor.transpose(bank[:, k, :], words[:, P * k : P * (k + 1)], ident[:])
+
+        def turn_copy(i):
+            grouped = work.tile([P, 2, 512], BF16, name="pg", align_bytes=64)
+            pg[i] = grouped
+            o = grouped[:].rearrange("p h x -> p (h x)").bitcast(F32).rearrange("p (h r u) -> p h r u", h=2, u=2)
+            if i < NB - 1:
+                nc.scalar.copy(out=o, in_=tb[i][0][:].rearrange("p (h u) r -> p h r u", h=2))
+            else:
+                for h, copy in ((0, nc.scalar.copy), (1, nc.vector.tensor_copy)):
+                    copy(out=o[:, h], in_=tb[i][h][:, 2 * h : 2 * h + 2, :].rearrange("p u r -> p r u"))
+
+        def p_quant(i):
+            codes = work.tile([P, 2, P], U32, name="pc", align_bytes=64)
+            for h in (0, 1):
+                nc.vector.quantize_mx(
+                    out=codes[:, h, :].bitcast(FP8X4),
+                    scales=pscale[:, h, P * i : P * (i + 1)],
+                    in_=pg[i][:, h, :],
+                )
+            nc.sync.dma_start(out=o1[:, :, P * i : P * (i + 1)], in_=codes[:].bitcast(I32))
+
+        def store_scales(lo, hi):
+            for q in range(4):
+                nc.sync.dma_start(
+                    out=o2[4 * q : 4 * q + 4, :, 32 * lo : 32 * hi],
+                    in_=pscale[32 * q : 32 * q + 4, :, P * lo : P * hi].bitcast(I32),
+                )
+
+        dgs = {0: d1_mul(0)}
+        d2_quant(*prev)
+        dgs[1] = d1_mul(1)
+        d1_quant(0, dgs[0])
+        c_mm(0)
+        for i in range(NB + 1):
+            if i + 1 < NB:
+                d1_quant(i + 1, dgs[i + 1])
+            if i < NB:
+                blend(i)
+            if i + 1 < NB:
+                c_mm(i + 1)
+            if i + 2 < NB:
+                dgs[i + 2] = d1_mul(i + 2)
+            if i == NB - 1:
+                cast(i)
+                turn_copy(i - 1)
+                turn(i)
+            else:
+                if i >= 1:
+                    turn_copy(i - 1)
+                if i < NB:
+                    cast(i)
+                    turn(i)
+            if i >= 1:
+                p_quant(i - 1)
+            if i == 7:
+                store_scales(0, 6)
+        store_scales(6, 8)

@@ -221,7 +221,7 @@ def tile_twotaskkroneckergradientcrossfactorema_x2_kernel(
             dg = work.tile([P, 2, 512], BF16, name="dg", align_bytes=64, bufs=4)
             for e in (0, 1):
                 k = 2 * j + e
-                if e == 0 and j >= 2:
+                if False:
                     d_mul_pool(k, dg[:, e, :])
                 else:
                     d_mul(k, dg[:, e, :])
@@ -242,7 +242,7 @@ def tile_twotaskkroneckergradientcrossfactorema_x2_kernel(
             dg = work.tile([P, 2, 512], BF16, name="dg", align_bytes=64, bufs=4)
             for g in (0, 1):
                 k = 16 + 2 * i + g
-                if g == 0:
+                if False:
                     d_mul_pool(k, dg[:, g, :])
                 else:
                     d_mul(k, dg[:, g, :])

@@ -16,6 +16,10 @@ ALU = mybir.AluOpType
 N, O, F = 1024, 512, 1024
 P = 128
 FLOPS = 2 * 2 * N * O * F + 2 * N * F * F
+LC = 1
+LOADS = "y21 a0 y10 a1 y11 w2 w1 a2 a3".split()
+FUNCS = "r0 s0 s1 r1 r2 r3 s2 s3".split()
+ORDER = """Y2.0.1 A Y2.1 Y1.0 Y1.1 S0 S1 D2.0.1 D1.2.0 D2.0.0 D1.1.0 D2.1.1 Q2.0 D1.0.0 S2 D2.1.0 F D2.2.1 S3 D2.2.0 D1.1.1 D2.3.0 D1.2.1 Q2.2 D1.0.1 D1.3.0 Q2.1 D1.3.1 D2.3.1 Q1.3 S4 Q1.1 Q1.2 Q2.3 Q1.0 S5 S6 S7 G2.4.0 G2.5.0 G1.4.1 R D2.7.1 D2.6.1 G1.5.0 D1.7.0 R G2.4.1 R D2.5.1 D2.7.0 R D2.6.0 Q2.5 Q2.4 Q2.6 Q2.7 G1.7.1 P0 D1.5.1 R R D1.4.0 G1.6.1 Q1.4 R Q1.5 R P1 D1.6.0 R P2 R Q1.6 Q1.7 R R R P4 R P3 X R P5 R""".split()
 NB = F // P
 
 
@@ -87,17 +91,15 @@ def tile_twotaskkroneckergradientcrossfactorema_x2_kernel(
                 )
 
         load_dy(2, 0, 2)
-        load_a(chunks[0])
         load_ws(2, nc.scalar)
         load_ws(1, nc.gpsimd)
-        load_dy(2, 1)
-        load_a(chunks[1])
-        load_dy(1, 0)
-        load_dy(1, 1)
-        load_w(2)
-        load_w(1)
-        load_a(chunks[2])
-        load_a(chunks[3])
+        for tok in LOADS:
+            if tok[0] == "y":
+                load_dy(int(tok[1]), int(tok[2]))
+            elif tok[0] == "a":
+                load_a(chunks[int(tok[1])])
+            else:
+                load_w(int(tok[1]))
         gv = g_old.rearrange("(b i p) f -> b p i f", p=P, i=4)
         for b in (0, 1):
             nc.sync.dma_start(out=gt[b][:], in_=gv[b])
@@ -108,17 +110,6 @@ def tile_twotaskkroneckergradientcrossfactorema_x2_kernel(
             nc.scalar.activation(out=o, in_=src, func=func, scale=scale)
 
         nc.scalar.activation(out=warm[:, 1:2], in_=warm[:, 0:1], func=ACT.Silu)
-        for c in chunks[:2]:
-            for pair in (0, 1):
-                act(c, pair, rt, ACT.Silu, -1.0)
-        for c in chunks:
-            for pair in (0, 1):
-                act(c, pair, st, ACT.Sigmoid, 1.0)
-        def silu_pair(p):
-            act(chunks[p // 2], p % 2, rt, ACT.Silu, -1.0)
-
-        silu_pair(4)
-
         def slope(c, pair):
             sl = slice(1024 * pair, 1024 * (pair + 1))
             nc.vector.scalar_tensor_tensor(
@@ -126,14 +117,14 @@ def tile_twotaskkroneckergradientcrossfactorema_x2_kernel(
                 op0=ALU.subtract, op1=ALU.mult,
             )
 
-        def dy_bank(t, g, b):
+        def dy_bank(t, g, b, copy=nc.vector.tensor_copy):
             bank = psum.tile([P, 2, 2, P], F32, name="tp", bufs=2)
             for k in (0, 1):
                 words = dyr[t, g][:, 2 * b + k, :].bitcast(F32)
                 for u in (0, 1):
                     nc.tensor.transpose(bank[:, k, u, :], words[:, u:256:2], ident[:])
             grouped = work.tile([P, 1024], BF16, name="dyg", align_bytes=64, bufs=4)
-            nc.vector.tensor_copy(
+            copy(
                 out=grouped[:].bitcast(F32).rearrange("p (t r u) -> p t r u", t=2, u=2),
                 in_=bank[:].rearrange("p t u r -> p t r u"),
             )
@@ -146,18 +137,21 @@ def tile_twotaskkroneckergradientcrossfactorema_x2_kernel(
                 in_=grouped[:],
             )
 
-        def dy_prep(t):
-            prev = None
-            for g in (0, 1):
-                for b in (0, 1):
-                    cur = (t, g, b, dy_bank(t, g, b))
-                    if prev:
-                        dy_quant(*prev)
-                    prev = cur
-            dy_quant(*prev)
+        def dy_prep(t, g, shared=0):
+            x0 = dy_bank(t, g, 0)
+            x1 = dy_bank(t, g, 1, nc.scalar.copy if shared else nc.vector.tensor_copy)
+            dy_quant(t, g, 0, x0)
+            dy_quant(t, g, 1, x1)
 
-        units = [(2, c[0], 4 * c[1] + j) for c in chunks for j in range(4)]
-        units += [(1, g, i) for i in range(NB) for g in (0, 1)]
+        units = []
+        for tok in ORDER:
+            if tok[0] in "DG":
+                x, y, z = [int(v) for v in tok[1:].split(".")]
+                if x == 2:
+                    units.append((2, chunks[y // 2][0], 4 * chunks[y // 2][1] + 2 * (y % 2) + z))
+                else:
+                    units.append((1, z, y))
+        pos = {u: k for k, u in enumerate(units)}
         banks = {}
 
         def mm1(k):
@@ -201,165 +195,219 @@ def tile_twotaskkroneckergradientcrossfactorema_x2_kernel(
             )
             nc.gpsimd.tensor_tensor(out=out, in0=tmp[:], in1=nm, op=ALU.mult)
 
-        dy_prep(2)
-        dy_prep(1)
-        for k in range(4):
-            mm1(k)
 
-        def d2_quant(j, dg):
-            t, g, fb = units[2 * j]
+        started = []
+        ready = set()
+
+        def feed(upto):
+            while len(started) < min(upto, len(units)):
+                k = len(started)
+                if units[k][:2] not in ready:
+                    return
+                mm1(k)
+                started.append(k)
+
+        def consume(u, out, pool=False):
+            k = pos[u]
+            feed(k + 1)
+            (d_mul_pool if pool else d_mul)(k, out)
+            feed(k + 5)
+
+        def d2_quant(j):
+            c = chunks[j // 2]
+            fb = 4 * c[1] + 2 * (j % 2)
             sl = slice(P * fb, P * (fb + 2))
             nc.vector.quantize_mx(
-                out=d2c[g][:, sl].bitcast(FP8X4),
-                scales=d2s[g][:, sl],
-                in_=dg[:].rearrange("p a b -> p (a b)"),
+                out=d2c[c[0]][:, sl].bitcast(FP8X4),
+                scales=d2s[c[0]][:, sl],
+                in_=dgs[2, j][:].rearrange("p a b -> p (a b)"),
             )
 
-        slope(chunks[0], 0)
-        prev = None
-        for j in range(8):
-            dg = work.tile([P, 2, 512], BF16, name="dg", align_bytes=64, bufs=4)
-            for e in (0, 1):
-                k = 2 * j + e
-                if False:
-                    d_mul_pool(k, dg[:, e, :])
-                else:
-                    d_mul(k, dg[:, e, :])
-                mm1(k + 4)
-            if 2 <= j < 5:
-                silu_pair(j + 3)
-            if j < 7:
-                slope(chunks[(j + 1) // 2], (j + 1) % 2)
-            if prev:
-                d2_quant(*prev)
-            prev = (j, dg)
-        cb, rr, rb, pg, tb, d1 = {}, {}, {}, {}, {}, {}
-        o0 = out_0.rearrange("(b p) f -> b p f", p=P)
-        o1 = out_1.bitcast(I32).rearrange("g p m o -> p g (m o)")
+        d1c = keep.tile([P, NB, 2, P], U32, name="d1c", align_bytes=64)
+        d1s = keep.tile([P, NB, 2, P], U8, name="d1s", align_bytes=64)
+        dgs = {}
+
+        def d1_quant(i):
+            nc.vector.quantize_mx(
+                out=d1c[:, i].rearrange("p a b -> p (a b)").bitcast(FP8X4),
+                scales=d1s[:, i].rearrange("p a b -> p (a b)"),
+                in_=dgs[1, i][:].rearrange("p a b -> p (a b)"),
+            )
+
+        def new_dg(key):
+            dgs[key] = work.tile([P, 2, 512], BF16, name="dg", align_bytes=64, bufs=7)
+
+        def take2(j, e, pool=False):
+            c = chunks[j // 2]
+            if (2, j) not in dgs:
+                new_dg((2, j))
+            consume((2, c[0], 4 * c[1] + 2 * (j % 2) + e), dgs[2, j][:, e, :], pool)
+
+        def take1(i, g, pool=False):
+            if (1, i) not in dgs:
+                new_dg((1, i))
+            consume((1, g, i), dgs[1, i][:, g, :], pool)
+
+        def slope_pair(j):
+            slope(chunks[j // 2], j % 2)
+
+        pairs = [(0, 0), (2, 0), (0, 1), (2, 1), (4, 0), (4, 1), (6, 0), (6, 1)]
+        cb, rr, rb, pg, tb = {}, {}, {}, {}, {}
+        o0 = out_0.rearrange("(b p) f -> p b f", p=P)
+        o1 = out_1.bitcast(I32).rearrange("g p m o -> g p (m o)")
         o2 = out_2.bitcast(I32).rearrange("g r m -> r g m")
 
-        def d1_mul(i):
-            dg = work.tile([P, 2, 512], BF16, name="dg", align_bytes=64, bufs=4)
+        def c_mm(n, e):
+            i, h = pairs[n][0] + e, pairs[n][1]
+            bank = psum.tile([P, 512], F32, name="cb", bufs=2)
             for g in (0, 1):
-                k = 16 + 2 * i + g
-                if False:
-                    d_mul_pool(k, dg[:, g, :])
-                else:
-                    d_mul(k, dg[:, g, :])
-                mm1(k + 4)
-            return dg
+                nc.tensor.matmul_mx(
+                    out=bank[:],
+                    lhsT=d1c[:, i, g, :].bitcast(FP8X4),
+                    lhsT_scale=d1s[:, i, g, :],
+                    rhs=d2c[g][:, 512 * h : 512 * (h + 1)].bitcast(FP8X4),
+                    rhs_scale=d2s[g][:, 512 * h : 512 * (h + 1)],
+                    start=(g == 0),
+                    stop=(g == 1),
+                )
+            cb[n, e] = bank
 
-        def d1_quant(i, dg):
-            codes = work.tile([P, 2, P], U32, name="d1c", align_bytes=64)
-            scales = work.tile([P, 2, P], U8, name="d1s", align_bytes=64)
-            nc.vector.quantize_mx(
-                out=codes[:].rearrange("p a b -> p (a b)").bitcast(FP8X4),
-                scales=scales[:].rearrange("p a b -> p (a b)"),
-                in_=dg[:].rearrange("p a b -> p (a b)"),
+        def blend(n, e):
+            i, h = pairs[n][0] + e, pairs[n][1]
+            if e == 0:
+                rr[n] = work.tile([P, 2, 512], F32, name="res", align_bytes=64, bufs=3)
+            sl = slice(512 * h, 512 * (h + 1))
+            nc.vector.scalar_tensor_tensor(
+                out=rr[n][:, e, :], in0=gt[i // 4][:, i % 4, sl], scalar=0.5, in1=cb[n, e][:],
+                op0=ALU.mult, op1=ALU.add,
             )
-            d1[i] = (codes, scales)
+            if e == 1:
+                nc.sync.dma_start(out=o0[:, i - 1 : i + 1, sl], in_=rr[n][:])
 
-        def c_mm(i):
-            codes, scales = d1[i]
-            for h in (0, 1):
-                bank = psum.tile([P, 512], F32, name="cb", bufs=2)
-                for g in (0, 1):
-                    nc.tensor.matmul_mx(
-                        out=bank[:],
-                        lhsT=codes[:, g, :].bitcast(FP8X4),
-                        lhsT_scale=scales[:, g, :],
-                        rhs=d2c[g][:, 512 * h : 512 * (h + 1)].bitcast(FP8X4),
-                        rhs_scale=d2s[g][:, 512 * h : 512 * (h + 1)],
-                        start=(g == 0),
-                        stop=(g == 1),
-                    )
-                cb[i, h] = bank
-
-        def blend(i):
-            res = work.tile([P, F], F32, name="res", align_bytes=64)
-            for h in (0, 1):
-                sl = slice(512 * h, 512 * (h + 1))
-                nc.vector.scalar_tensor_tensor(
-                    out=res[:, sl], in0=gt[i // 4][:, i % 4, sl], scalar=0.5, in1=cb[i, h][:],
-                    op0=ALU.mult, op1=ALU.add,
-                )
-            nc.sync.dma_start(out=o0[i], in_=res[:])
-            rr[i] = res
-
-        def cast(i):
-            b16 = work.tile([P, 2, 512], BF16, name="b16", align_bytes=64)
-            rb[i] = b16
-            for h in (0, 1):
-                o = b16[:, h, :].rearrange("q (u p e) -> q u p e", u=2, e=2)
-                src = rr[i][:, 512 * h : 512 * (h + 1)].rearrange("q (p u e) -> q u p e", u=2, e=2)
-                if i == NB - 1 and h == 1:
-                    nc.vector.tensor_copy(out=o, in_=src)
-                else:
-                    nc.scalar.activation(out=o, in_=src, func=ACT.Copy)
-
-        def turn(i):
-            last = i == NB - 1
-            words = rb[i][:].rearrange("q h x -> q (h x)").bitcast(F32)
-            tb[i] = []
-            for k in range(4):
-                if k == 0 or (last and k == 2):
-                    bank = psum.tile([P, 4, P], F32, name="tp", bufs=2)
-                    tb[i].append(bank)
-                nc.tensor.transpose(bank[:, k, :], words[:, P * k : P * (k + 1)], ident[:])
-
-        def turn_copy(i):
-            grouped = work.tile([P, 2, 512], BF16, name="pg", align_bytes=64)
-            pg[i] = grouped
-            o = grouped[:].rearrange("p h x -> p (h x)").bitcast(F32).rearrange("p (h r u) -> p h r u", h=2, u=2)
-            if i < NB - 1:
-                nc.scalar.copy(out=o, in_=tb[i][0][:].rearrange("p (h u) r -> p h r u", h=2))
+        def cast(n, e, vec=False):
+            if e == 0:
+                rb[n] = work.tile([P, 2, 512], BF16, name="b16", align_bytes=64)
+            o = rb[n][:, e, :].rearrange("q (u p e) -> q u p e", u=2, e=2)
+            src = rr[n][:, e, :].rearrange("q (p u e) -> q u p e", u=2, e=2)
+            if vec:
+                nc.vector.tensor_copy(out=o, in_=src)
             else:
-                for h, copy in ((0, nc.scalar.copy), (1, nc.vector.tensor_copy)):
-                    copy(out=o[:, h], in_=tb[i][h][:, 2 * h : 2 * h + 2, :].rearrange("p u r -> p r u"))
+                nc.scalar.activation(out=o, in_=src, func=ACT.Copy)
 
-        def p_quant(i):
-            codes = work.tile([P, 2, P], U32, name="pc", align_bytes=64)
-            for h in (0, 1):
+        def turn(n, e, own=False):
+            if e == 0 or own:
+                bank = psum.tile([P, 4, P], F32, name="tp", bufs=2)
+                tb[n, e] = bank
+            else:
+                tb[n, e] = tb[n, 0]
+            words = rb[n][:, e, :].bitcast(F32)
+            for k in (0, 1):
+                nc.tensor.transpose(tb[n, e][:, 2 * e + k, :], words[:, P * k : P * (k + 1)], ident[:])
+
+        def turn_copy(n):
+            pg[n] = work.tile([P, 2, 512], BF16, name="pg", align_bytes=64)
+            o = pg[n][:].rearrange("p e x -> p (e x)").bitcast(F32)
+            nc.scalar.copy(
+                out=o.rearrange("p (e r u) -> p e r u", e=2, u=2),
+                in_=tb[n, 0][:].rearrange("p (e u) r -> p e r u", e=2),
+            )
+
+        def turn_copy_half(n, e, copy):
+            if e == 0:
+                pg[n] = work.tile([P, 2, 512], BF16, name="pg", align_bytes=64)
+            copy(
+                out=pg[n][:, e, :].bitcast(F32).rearrange("p (r u) -> p r u", u=2),
+                in_=tb[n, e][:, 2 * e : 2 * e + 2, :].rearrange("p u r -> p r u"),
+            )
+
+        def p_quant(n, parts=1):
+            i, h = pairs[n]
+            codes = work.tile([P, 2 * P], U32, name="pc", align_bytes=64)
+            w = 2 * P // parts
+            src = pg[n][:].rearrange("p e x -> p (e x)")
+            for k in range(parts):
                 nc.vector.quantize_mx(
-                    out=codes[:, h, :].bitcast(FP8X4),
-                    scales=pscale[:, h, P * i : P * (i + 1)],
-                    in_=pg[i][:, h, :],
+                    out=codes[:, w * k : w * (k + 1)].bitcast(FP8X4),
+                    scales=pscale[:, h, P * i + w * k : P * i + w * (k + 1)],
+                    in_=src[:, 4 * w * k : 4 * w * (k + 1)],
                 )
-            nc.sync.dma_start(out=o1[:, :, P * i : P * (i + 1)], in_=codes[:].bitcast(I32))
+            nc.sync.dma_start(out=o1[h, :, P * i : P * (i + 2)], in_=codes[:].bitcast(I32))
 
-        def store_scales(lo, hi):
+        def store_scales(lo, hi, engs):
             for q in range(4):
-                nc.sync.dma_start(
+                engs[q % len(engs)].dma_start(
                     out=o2[4 * q : 4 * q + 4, :, 32 * lo : 32 * hi],
                     in_=pscale[32 * q : 32 * q + 4, :, P * lo : P * hi].bitcast(I32),
                 )
 
-        dgs = {0: d1_mul(0)}
-        d2_quant(*prev)
-        dgs[1] = d1_mul(1)
-        d1_quant(0, dgs[0])
-        c_mm(0)
-        for i in range(NB + 1):
-            if i + 1 < NB:
-                d1_quant(i + 1, dgs[i + 1])
-            if i < NB:
-                blend(i)
-            if i + 1 < NB:
-                c_mm(i + 1)
-            if i + 2 < NB:
-                dgs[i + 2] = d1_mul(i + 2)
-            if i == NB - 1:
-                cast(i)
-                turn_copy(i - 1)
-                turn(i)
+        seq = [(n, e) for n in range(8) for e in (0, 1)]
+        state = {"c": 0, "b": 0}
+        done1, done2 = set(), set()
+
+        def pump():
+            while state["c"] < min(16, state["b"] + 2):
+                n, e = seq[state["c"]]
+                i, h = pairs[n][0] + e, pairs[n][1]
+                if i not in done1 or not all([4 * h + q in done2 for q in range(4)]):
+                    return
+                c_mm(n, e)
+                state["c"] += 1
+
+        def q1(i):
+            d1_quant(i)
+            done1.add(i)
+            pump()
+
+        def q2(j):
+            d2_quant(j)
+            done2.add(j)
+            pump()
+
+        def R():
+            r = state["b"]
+            n, e = seq[r]
+            blend(n, e)
+            state["b"] += 1
+            pump()
+            last = r == 15
+            if r >= 1:
+                tn, tz = seq[r - 1]
+                turn(tn, tz)
+            if e == LC and n >= 1:
+                turn_copy(n - 1)
+            cast(n, e, last)
+
+        consumed = 0
+        for tok in ORDER:
+            arg = [int(v) for v in tok[1:].split(".") if v]
+            if tok[0] == "Y":
+                dy_prep(*arg)
+                ready.add((arg[0], arg[1]))
+            elif tok[0] == "F":
+                feed(4)
+            elif tok[0] == "A":
+                for fn in FUNCS:
+                    for pair in (0, 1):
+                        if fn[0] == "r":
+                            act(chunks[int(fn[1])], pair, rt, ACT.Silu, -1.0)
+                        else:
+                            act(chunks[int(fn[1])], pair, st, ACT.Sigmoid, 1.0)
+            elif tok[0] == "S":
+                slope_pair(*arg)
+            elif tok[0] in "DG":
+                (take2 if arg[0] == 2 else take1)(arg[1], arg[2], tok[0] == "G")
+                consumed += 1
+            elif tok[0] == "Q":
+                (q2 if arg[0] == 2 else q1)(arg[1])
+            elif tok[0] == "R":
+                R()
+            elif tok[0] == "P":
+                p_quant(*arg)
             else:
-                if i >= 1:
-                    turn_copy(i - 1)
-                if i < NB:
-                    cast(i)
-                    turn(i)
-            if i >= 1:
-                p_quant(i - 1)
-            if i == 7:
-                store_scales(0, 6)
-        store_scales(6, 8)
+                store_scales(0, 4, [nc.sync])
+        turn(7, 1, True)
+        p_quant(6)
+        turn_copy_half(7, 0, nc.scalar.copy)
+        turn_copy_half(7, 1, nc.vector.tensor_copy)
+        p_quant(7, 2)
+        store_scales(4, 8, [nc.sync, nc.scalar])

@@ -15,21 +15,35 @@ ALU = mybir.AluOpType
 
 N, O, F = 1024, 512, 1024
 P = 128
-FLOPS = 2 * 2 * N * O * F + 2 * N * F * F
-LC = 1
-LOADS = "y21 a0 y10 a1 y11 w2 w1 a2 a3".split()
-FUNCS = "r0 s0 s1 r1 r2 r3 s2 s3".split()
-ORDER = """Y2.0.1 A Y2.1 Y1.0 Y1.1 S0 S1 D2.0.1 D1.2.0 D2.0.0 D1.1.0 D2.1.1 Q2.0 D1.0.0 S2 D2.1.0 F D2.2.1 S3 D2.2.0 D1.1.1 D2.3.0 D1.2.1 Q2.2 D1.0.1 D1.3.0 Q2.1 D1.3.1 D2.3.1 Q1.3 S4 Q1.1 Q1.2 Q2.3 Q1.0 S5 S6 S7 G2.4.0 G2.5.0 G1.4.1 R D2.7.1 D2.6.1 G1.5.0 D1.7.0 R G2.4.1 R D2.5.1 D2.7.0 R D2.6.0 Q2.5 Q2.4 Q2.6 Q2.7 G1.7.1 P0 D1.5.1 R R D1.4.0 G1.6.1 Q1.4 R Q1.5 R P1 D1.6.0 R P2 R Q1.6 Q1.7 R R R P4 R P3 X R P5 R""".split()
+PACK = 4
+GROUP = P * PACK
 NB = F // P
+FLOPS = 2 * 2 * N * O * F + 2 * N * F * F
+
+SLOPE_FACTOR = {1: -1.0 / (2 * N), 2: -1.0}
+
+CHUNKS = [(0, 0), (1, 0), (0, 1), (1, 1)]
+
+PAIRS = [(0, 0), (2, 0), (0, 1), (2, 1), (4, 0), (4, 1), (6, 0), (6, 1)]
+
+LOADS = "a0 y10 a1 y21 w2 a3 y11 a2 w1".split()
+
+ORDER = """
+Y2.0.1.0 s0.1 q2.0.1 s0.0 Y2.0.0.0 U1 s1.1 Y1.0.0.1 Y1.0.1.1 s1.0 U0 Y2.1.1.1 S1 U3 q1.0.1 r3.0 q2.0.0 q1.0.0 S3
+F Y2.1.0.1 U2 q2.1.1 Y1.1.0.1 D2.1.1 D2.1.0 r2.1 q2.1.0 S0 S2 q1.1.0 Y1.1.1.1 G2.2.1 D2.0.0 D1.0.0 r2.0 D1.1.0
+q1.1.1 G2.2.0 r3.1 D2.0.1 D2.3.0 G1.3.0 D1.3.1 D1.0.1 s3.0 D2.3.1 Q2.0 Q2.3 Q2.2 Q1.3 Q1.0 Q2.1 s2.0 S6 S4
+D1.1.1 D2.6.0 G1.2.0 s2.1 S5 G1.4.0 s3.1 D2.4.1 G1.2.1 D2.4.0 D2.6.1 R Q1.1 Q1.2 S7 G2.5.1 G2.7.1 D2.5.0 R R
+D2.7.0 Q2.4 Q2.6 Q2.5 Q2.7 G1.7.1 R D1.4.1 G1.7.0 Q1.4 G1.5.0 R G1.6.1 R D1.6.0 D1.5.1 R R P1 Q1.5 P0 R Q1.7 V R
+Q1.6 R P2 P3 R P4 V R R X P5
+""".split()
 
 
 def tile_twotaskkroneckergradientcrossfactorema_x2_kernel(
     tc, dy1, w1_words, w1_scales, dy2, w2_words, w2_scales, a, g_old, out_0, out_1, out_2
 ):
     nc = tc.nc
-    dy_in = {1: dy1, 2: dy2}
-    w_in = {1: (w1_words, w1_scales), 2: (w2_words, w2_scales)}
-    d_scale = {1: -1.0 / 2048.0, 2: -1.0}
+    dy_rows = {1: dy1, 2: dy2}
+    w_bytes = {1: (w1_words, w1_scales), 2: (w2_words, w2_scales)}
 
     with ExitStack() as ctx:
         keep = ctx.enter_context(tc.tile_pool(name="keep", bufs=1))
@@ -42,372 +56,339 @@ def tile_twotaskkroneckergradientcrossfactorema_x2_kernel(
 
         ctx.enter_context(tc.manual_schedule())
 
-        dyr, dyc, dys, ww, ws = {}, {}, {}, {}, {}
+        dy_raw, dy_codes, dy_scales, w_codes, w_plane = {}, {}, {}, {}, {}
         for t in (1, 2):
-            ww[t] = keep.tile([P, 2 * F], U8, name="ww%d" % t, align_bytes=64)
-            ws[t] = keep.tile([P, F], U8, name="ws%d" % t, align_bytes=64)
+            w_codes[t] = keep.tile([P, 2 * F], U8, name="w_codes%d" % t, align_bytes=64)
+            w_plane[t] = keep.tile([P, F], U8, name="w_plane%d" % t, align_bytes=64)
             for g in (0, 1):
-                dyr[t, g] = keep.tile([P, 4, O], BF16, name="dyr%d%d" % (t, g), align_bytes=64)
-                dyc[t, g] = keep.tile([P, 512], U32, name="dyc%d%d" % (t, g), align_bytes=64)
-                dys[t, g] = keep.tile([P, 512], U8, name="dys%d%d" % (t, g), align_bytes=64)
-        chunks = [(0, 0), (1, 0), (0, 1), (1, 1)]
-        at, st, rt = {}, {}, {}
-        for c in chunks:
-            at[c] = keep.tile([P, 4, 512], BF16, name="a%d%d" % c, align_bytes=64)
-            st[c] = keep.tile([P, 2048], F32, name="s%d%d" % c, align_bytes=64)
-            rt[c] = keep.tile([P, 2048], F32, name="r%d%d" % c, align_bytes=64)
-        gt = {}
+                dy_raw[t, g] = keep.tile([P, PACK, O], BF16, name="dy_raw%d%d" % (t, g), align_bytes=64)
+                dy_codes[t, g] = keep.tile([P, GROUP], U32, name="dy_codes%d%d" % (t, g), align_bytes=64)
+                dy_scales[t, g] = keep.tile([P, GROUP], U8, name="dy_scales%d%d" % (t, g), align_bytes=64)
+        a_raw, sig, slo = {}, {}, {}
+        for c in CHUNKS:
+            a_raw[c] = keep.tile([P, PACK, F // 2], BF16, name="a_raw%d%d" % c, align_bytes=64)
+            sig[c] = keep.tile([P, PACK * F // 2], F32, name="sig%d%d" % c, align_bytes=64)
+            slo[c] = keep.tile([P, PACK * F // 2], F32, name="slo%d%d" % c, align_bytes=64)
+        g_rows = {}
         for b in (0, 1):
-            gt[b] = keep.tile([P, 4, F], BF16, name="gt%d" % b, align_bytes=64)
-        d2c, d2s = {}, {}
+            g_rows[b] = keep.tile([P, 4, F], BF16, name="g_rows%d" % b, align_bytes=64)
+        d2_codes, d2_scales = {}, {}
         for g in (0, 1):
-            d2c[g] = keep.tile([P, F], U32, name="d2c%d" % g, align_bytes=64)
-            d2s[g] = keep.tile([P, F], U8, name="d2s%d" % g, align_bytes=64)
-        pscale = keep.tile([P, 2, F], U8, name="pscale", align_bytes=64)
+            d2_codes[g] = keep.tile([P, F], U32, name="d2_codes%d" % g, align_bytes=64)
+            d2_scales[g] = keep.tile([P, F], U8, name="d2_scales%d" % g, align_bytes=64)
+        p_scales = keep.tile([P, 2, F], U8, name="p_scales", align_bytes=64)
+        d1_codes = keep.tile([P, NB, 2, P], U32, name="d1_codes", align_bytes=64)
+        d1_scales = keep.tile([P, NB, 2, P], U8, name="d1_scales", align_bytes=64)
 
-        nc.vector.memset(ws[2][:].bitcast(I32), 0)
+        nc.vector.memset(w_plane[2][:].bitcast(I32), 0)
         nc.vector.memset(warm[:], 0.0)
-        nc.vector.memset(ws[1][:].bitcast(I32), 0)
+        nc.vector.memset(w_plane[1][:].bitcast(I32), 0)
 
         def load_dy(t, g, parts=1):
-            v = dy_in[t].rearrange("(g p t) o -> g p t o", p=P, t=4)
-            n = 4 // parts
-            for k in range(0, 4, n):
-                nc.sync.dma_start(out=dyr[t, g][:, k : k + n, :], in_=v[g, :, k : k + n, :])
+            rows = dy_rows[t].rearrange("(g p t) o -> g p t o", p=P, t=PACK)
+            n = PACK // parts
+            for k in range(0, PACK, n):
+                nc.sync.dma_start(out=dy_raw[t, g][:, k : k + n, :], in_=rows[g, :, k : k + n, :])
 
         def load_a(c):
             g, h = c
-            v = a.rearrange("(g p t) f -> g p t f", p=P, t=4)
-            nc.sync.dma_start(out=at[c][:], in_=v[g, :, :, 512 * h : 512 * (h + 1)])
+            rows = a.rearrange("(g p t) f -> g p t f", p=P, t=PACK)
+            nc.sync.dma_start(out=a_raw[c][:], in_=rows[g, :, :, F // 2 * h : F // 2 * (h + 1)])
 
-        def load_w(t):
-            nc.sync.dma_start(out=ww[t][:].bitcast(I32), in_=w_in[t][0][0].bitcast(I32))
-
-        def load_ws(t, eng):
+        def load_w_scales(t, queue):
             for q in range(4):
-                eng.dma_start(
-                    out=ws[t][32 * q : 32 * q + 4, :].bitcast(I32),
-                    in_=w_in[t][1][0, 4 * q : 4 * q + 4, :].bitcast(I32),
+                queue.dma_start(
+                    out=w_plane[t][32 * q : 32 * q + 4, :].bitcast(I32),
+                    in_=w_bytes[t][1][0, 4 * q : 4 * q + 4, :].bitcast(I32),
                 )
 
         load_dy(2, 0, 2)
-        load_ws(2, nc.scalar)
-        load_ws(1, nc.gpsimd)
+        load_w_scales(2, nc.scalar)
         for tok in LOADS:
             if tok[0] == "y":
                 load_dy(int(tok[1]), int(tok[2]))
             elif tok[0] == "a":
-                load_a(chunks[int(tok[1])])
+                load_a(CHUNKS[int(tok[1])])
             else:
-                load_w(int(tok[1]))
-        gv = g_old.rearrange("(b i p) f -> b p i f", p=P, i=4)
+                t = int(tok[1])
+                nc.sync.dma_start(out=w_codes[t][:].bitcast(I32), in_=w_bytes[t][0][0].bitcast(I32))
+                if t == 1:
+                    load_w_scales(1, nc.sync)
+        g_view = g_old.rearrange("(b i p) f -> b p i f", p=P, i=4)
         for b in (0, 1):
-            nc.sync.dma_start(out=gt[b][:], in_=gv[b])
+            nc.sync.dma_start(out=g_rows[b][:], in_=g_view[b])
 
-        def act(c, pair, dst, func, scale):
-            src = at[c][:, :, 256 * pair : 256 * (pair + 1)].rearrange("p t f -> p f t")
-            o = dst[c][:, 1024 * pair : 1024 * (pair + 1)].rearrange("p (f t) -> p f t", t=4)
-            nc.scalar.activation(out=o, in_=src, func=func, scale=scale)
+        nc.scalar.activation(out=warm[:, 1:2], in_=warm[:, 0:1], func=ACT.Sigmoid)
 
-        nc.scalar.activation(out=warm[:, 1:2], in_=warm[:, 0:1], func=ACT.Silu)
-        def slope(c, pair):
-            sl = slice(1024 * pair, 1024 * (pair + 1))
+        def tile_of(c, half):
+            return slice(PACK * 256 * half, PACK * 256 * (half + 1))
+
+        def by_feature(view):
+            return view.rearrange("p (f t) -> p f t", t=PACK)
+
+        def a_by_feature(c, half):
+            return a_raw[c][:, :, 256 * half : 256 * (half + 1)].rearrange("p t f -> p f t")
+
+        def activate(c, half, dst, func, scale):
+            nc.scalar.activation(
+                out=by_feature(dst[c][:, tile_of(c, half)]), in_=a_by_feature(c, half), func=func, scale=scale
+            )
+
+        def silu_by_vector(c, half):
+            sl = tile_of(c, half)
             nc.vector.scalar_tensor_tensor(
-                out=rt[c][:, sl], in0=rt[c][:, sl], scalar=1.0, in1=st[c][:, sl],
+                out=by_feature(slo[c][:, sl]), in0=by_feature(sig[c][:, sl]), scalar=1.0, in1=a_by_feature(c, half),
                 op0=ALU.subtract, op1=ALU.mult,
             )
 
-        def dy_bank(t, g, b, copy=nc.vector.tensor_copy):
-            bank = psum.tile([P, 2, 2, P], F32, name="tp", bufs=2)
+        def slope(c, half):
+            sl = tile_of(c, half)
+            nc.vector.scalar_tensor_tensor(
+                out=slo[c][:, sl], in0=slo[c][:, sl], scalar=1.0, in1=sig[c][:, sl], op0=ALU.subtract, op1=ALU.mult
+            )
+
+        dy_grouped = {}
+
+        def turn_dy(t, g, b, copy):
+            bank = psum.tile([P, 2, 2, P], F32, name="turned", bufs=2)
             for k in (0, 1):
-                words = dyr[t, g][:, 2 * b + k, :].bitcast(F32)
+                words = dy_raw[t, g][:, 2 * b + k, :].bitcast(F32)
                 for u in (0, 1):
-                    nc.tensor.transpose(bank[:, k, u, :], words[:, u:256:2], ident[:])
-            grouped = work.tile([P, 1024], BF16, name="dyg", align_bytes=64, bufs=4)
+                    nc.tensor.transpose(bank[:, k, u, :], words[:, u : O // 2 : 2], ident[:])
+            grouped = work.tile([P, 2 * P * PACK], BF16, name="dy_grouped", align_bytes=64, bufs=4)
             copy(
                 out=grouped[:].bitcast(F32).rearrange("p (t r u) -> p t r u", t=2, u=2),
                 in_=bank[:].rearrange("p t u r -> p t r u"),
             )
-            return grouped
+            dy_grouped[t, g, b] = grouped
 
-        def dy_quant(t, g, b, grouped):
+        def quantize_dy(t, g, b):
+            cols = slice(2 * P * b, 2 * P * (b + 1))
             nc.vector.quantize_mx(
-                out=dyc[t, g][:, 256 * b : 256 * (b + 1)].bitcast(FP8X4),
-                scales=dys[t, g][:, 256 * b : 256 * (b + 1)],
-                in_=grouped[:],
+                out=dy_codes[t, g][:, cols].bitcast(FP8X4),
+                scales=dy_scales[t, g][:, cols],
+                in_=dy_grouped[t, g, b][:],
             )
-
-        def dy_prep(t, g, shared=0):
-            x0 = dy_bank(t, g, 0)
-            x1 = dy_bank(t, g, 1, nc.scalar.copy if shared else nc.vector.tensor_copy)
-            dy_quant(t, g, 0, x0)
-            dy_quant(t, g, 1, x1)
 
         units = []
         for tok in ORDER:
             if tok[0] in "DG":
-                x, y, z = [int(v) for v in tok[1:].split(".")]
-                if x == 2:
-                    units.append((2, chunks[y // 2][0], 4 * chunks[y // 2][1] + 2 * (y % 2) + z))
+                t, x, y = [int(v) for v in tok[1:].split(".")]
+                if t == 2:
+                    g, h = CHUNKS[x // 2]
+                    units.append((2, g, 4 * h + 2 * (x % 2) + y))
                 else:
-                    units.append((1, z, y))
-        pos = {u: k for k, u in enumerate(units)}
+                    units.append((1, y, x))
+        position = {u: k for k, u in enumerate(units)}
         banks = {}
+        quantized_dy = set()
 
-        def mm1(k):
-            if k >= len(units):
-                return
+        def multiply(k):
             t, g, fb = units[k]
-            bank = psum.tile([P, 4, P], F32, name="s1", bufs=4)
-            for q in range(4):
+            bank = psum.tile([P, PACK, P], F32, name="unit", bufs=4)
+            for q in range(PACK):
                 nc.tensor.matmul_mx(
                     out=bank[:, q, :],
-                    lhsT=dyc[t, g][:, P * q : P * (q + 1)].bitcast(FP8X4),
-                    lhsT_scale=dys[t, g][:, P * q : P * (q + 1)],
-                    rhs=ww[t][:, 256 * fb : 256 * (fb + 1)].bitcast(FP4X4),
-                    rhs_scale=ws[t][:, P * fb : P * (fb + 1)],
+                    lhsT=dy_codes[t, g][:, P * q : P * (q + 1)].bitcast(FP8X4),
+                    lhsT_scale=dy_scales[t, g][:, P * q : P * (q + 1)],
+                    rhs=w_codes[t][:, 2 * P * fb : 2 * P * (fb + 1)].bitcast(FP4X4),
+                    rhs_scale=w_plane[t][:, P * fb : P * (fb + 1)],
                     start=True,
                     stop=True,
                 )
             banks[k] = bank
 
-        def d_mul(k, out):
-            t, g, fb = units[k]
-            nm = rt[g, fb // 4][:, 512 * (fb % 4) : 512 * (fb % 4 + 1)]
-            nc.vector.scalar_tensor_tensor(
-                out=out.rearrange("p (f t) -> p f t", t=4),
-                in0=nm.rearrange("p (f t) -> p f t", t=4),
-                scalar=d_scale[t],
-                in1=banks[k][:].rearrange("p t f -> p f t"),
-                op0=ALU.mult,
-                op1=ALU.mult,
-            )
-
-        def d_mul_pool(k, out):
-            t, g, fb = units[k]
-            nm = rt[g, fb // 4][:, 512 * (fb % 4) : 512 * (fb % 4 + 1)]
-            tmp = work.tile([P, 512], F32, name="tmp", align_bytes=64)
-            nc.scalar.activation(
-                out=tmp[:].rearrange("p (f t) -> p f t", t=4),
-                in_=banks[k][:].rearrange("p t f -> p f t"),
-                func=ACT.Copy,
-                scale=d_scale[t],
-            )
-            nc.gpsimd.tensor_tensor(out=out, in0=tmp[:], in1=nm, op=ALU.mult)
-
-
-        started = []
-        ready = set()
-
         def feed(upto):
-            while len(started) < min(upto, len(units)):
-                k = len(started)
-                if units[k][:2] not in ready:
+            while len(banks) < min(upto, len(units)):
+                t, g, fb = units[len(banks)]
+                if (t, g, 0) not in quantized_dy or (t, g, 1) not in quantized_dy:
                     return
-                mm1(k)
-                started.append(k)
+                multiply(len(banks))
 
-        def consume(u, out, pool=False):
-            k = pos[u]
+        def apply_slope(k, out, by_gpsimd):
+            t, g, fb = units[k]
+            slope_part = slo[g, fb // 4][:, PACK * P * (fb % 4) : PACK * P * (fb % 4 + 1)]
+            product = banks[k][:].rearrange("p t f -> p f t")
+            if by_gpsimd:
+                copied = work.tile([P, PACK * P], F32, name="copied", align_bytes=64)
+                nc.scalar.activation(out=by_feature(copied[:]), in_=product, func=ACT.Copy, scale=SLOPE_FACTOR[t])
+                nc.gpsimd.tensor_tensor(out=out, in0=copied[:], in1=slope_part, op=ALU.mult)
+            else:
+                nc.vector.scalar_tensor_tensor(
+                    out=by_feature(out), in0=by_feature(slope_part), scalar=SLOPE_FACTOR[t], in1=product,
+                    op0=ALU.mult, op1=ALU.mult,
+                )
+
+        d_grouped = {}
+
+        def unit(t, x, y, by_gpsimd):
+            if (t, x) not in d_grouped:
+                d_grouped[t, x] = work.tile([P, 2, PACK * P], BF16, name="d_grouped", align_bytes=64, bufs=7)
+            k = len(started)
+            started.append(k)
             feed(k + 1)
-            (d_mul_pool if pool else d_mul)(k, out)
+            apply_slope(k, d_grouped[t, x][:, y, :], by_gpsimd)
             feed(k + 5)
 
-        def d2_quant(j):
-            c = chunks[j // 2]
-            fb = 4 * c[1] + 2 * (j % 2)
-            sl = slice(P * fb, P * (fb + 2))
+        started = []
+
+        def quantize_d(t, x):
+            if t == 2:
+                g, h = CHUNKS[x // 2]
+                first = P * (4 * h + 2 * (x % 2))
+                codes, scales = d2_codes[g][:, first : first + 2 * P], d2_scales[g][:, first : first + 2 * P]
+            else:
+                codes = d1_codes[:, x].rearrange("p g f -> p (g f)")
+                scales = d1_scales[:, x].rearrange("p g f -> p (g f)")
             nc.vector.quantize_mx(
-                out=d2c[c[0]][:, sl].bitcast(FP8X4),
-                scales=d2s[c[0]][:, sl],
-                in_=dgs[2, j][:].rearrange("p a b -> p (a b)"),
+                out=codes.bitcast(FP8X4), scales=scales, in_=d_grouped[t, x][:].rearrange("p a b -> p (a b)")
             )
 
-        d1c = keep.tile([P, NB, 2, P], U32, name="d1c", align_bytes=64)
-        d1s = keep.tile([P, NB, 2, P], U8, name="d1s", align_bytes=64)
-        dgs = {}
-
-        def d1_quant(i):
-            nc.vector.quantize_mx(
-                out=d1c[:, i].rearrange("p a b -> p (a b)").bitcast(FP8X4),
-                scales=d1s[:, i].rearrange("p a b -> p (a b)"),
-                in_=dgs[1, i][:].rearrange("p a b -> p (a b)"),
-            )
-
-        def new_dg(key):
-            dgs[key] = work.tile([P, 2, 512], BF16, name="dg", align_bytes=64, bufs=7)
-
-        def take2(j, e, pool=False):
-            c = chunks[j // 2]
-            if (2, j) not in dgs:
-                new_dg((2, j))
-            consume((2, c[0], 4 * c[1] + 2 * (j % 2) + e), dgs[2, j][:, e, :], pool)
-
-        def take1(i, g, pool=False):
-            if (1, i) not in dgs:
-                new_dg((1, i))
-            consume((1, g, i), dgs[1, i][:, g, :], pool)
-
-        def slope_pair(j):
-            slope(chunks[j // 2], j % 2)
-
-        pairs = [(0, 0), (2, 0), (0, 1), (2, 1), (4, 0), (4, 1), (6, 0), (6, 1)]
-        cb, rr, rb, pg, tb = {}, {}, {}, {}, {}
         o0 = out_0.rearrange("(b p) f -> p b f", p=P)
         o1 = out_1.bitcast(I32).rearrange("g p m o -> g p (m o)")
         o2 = out_2.bitcast(I32).rearrange("g r m -> r g m")
+        out_tiles = [(n, e) for n in range(NB) for e in (0, 1)]
+        products, result, rounded, turned, p_grouped = {}, {}, {}, {}, {}
+        blended = []
+        quantized_d = set()
 
-        def c_mm(n, e):
-            i, h = pairs[n][0] + e, pairs[n][1]
-            bank = psum.tile([P, 512], F32, name="cb", bufs=2)
+        def second_stage(n, e):
+            i, h = PAIRS[n][0] + e, PAIRS[n][1]
+            bank = psum.tile([P, F // 2], F32, name="product", bufs=2)
             for g in (0, 1):
                 nc.tensor.matmul_mx(
                     out=bank[:],
-                    lhsT=d1c[:, i, g, :].bitcast(FP8X4),
-                    lhsT_scale=d1s[:, i, g, :],
-                    rhs=d2c[g][:, 512 * h : 512 * (h + 1)].bitcast(FP8X4),
-                    rhs_scale=d2s[g][:, 512 * h : 512 * (h + 1)],
+                    lhsT=d1_codes[:, i, g, :].bitcast(FP8X4),
+                    lhsT_scale=d1_scales[:, i, g, :],
+                    rhs=d2_codes[g][:, F // 2 * h : F // 2 * (h + 1)].bitcast(FP8X4),
+                    rhs_scale=d2_scales[g][:, F // 2 * h : F // 2 * (h + 1)],
                     start=(g == 0),
                     stop=(g == 1),
                 )
-            cb[n, e] = bank
+            products[n, e] = bank
+
+        def pump():
+            while len(products) < min(len(out_tiles), len(blended) + 2):
+                n, e = out_tiles[len(products)]
+                i, h = PAIRS[n][0] + e, PAIRS[n][1]
+                if (1, i) not in quantized_d or not all([(2, 4 * h + q) in quantized_d for q in range(4)]):
+                    return
+                second_stage(n, e)
 
         def blend(n, e):
-            i, h = pairs[n][0] + e, pairs[n][1]
+            i, h = PAIRS[n][0] + e, PAIRS[n][1]
+            cols = slice(F // 2 * h, F // 2 * (h + 1))
             if e == 0:
-                rr[n] = work.tile([P, 2, 512], F32, name="res", align_bytes=64, bufs=3)
-            sl = slice(512 * h, 512 * (h + 1))
+                result[n] = work.tile([P, 2, F // 2], F32, name="result", align_bytes=64)
             nc.vector.scalar_tensor_tensor(
-                out=rr[n][:, e, :], in0=gt[i // 4][:, i % 4, sl], scalar=0.5, in1=cb[n, e][:],
+                out=result[n][:, e, :], in0=g_rows[i // 4][:, i % 4, cols], scalar=0.5, in1=products[n, e][:],
                 op0=ALU.mult, op1=ALU.add,
             )
             if e == 1:
-                nc.sync.dma_start(out=o0[:, i - 1 : i + 1, sl], in_=rr[n][:])
+                nc.sync.dma_start(out=o0[:, i - 1 : i + 1, cols], in_=result[n][:])
 
-        def cast(n, e, vec=False):
+        def round_result(n, e, by_vector):
             if e == 0:
-                rb[n] = work.tile([P, 2, 512], BF16, name="b16", align_bytes=64)
-            o = rb[n][:, e, :].rearrange("q (u p e) -> q u p e", u=2, e=2)
-            src = rr[n][:, e, :].rearrange("q (p u e) -> q u p e", u=2, e=2)
-            if vec:
-                nc.vector.tensor_copy(out=o, in_=src)
+                rounded[n] = work.tile([P, 2, F // 2], BF16, name="rounded", align_bytes=64)
+            dst = rounded[n][:, e, :].rearrange("q (u p w) -> q u p w", u=2, w=2)
+            src = result[n][:, e, :].rearrange("q (p u w) -> q u p w", u=2, w=2)
+            if by_vector:
+                nc.vector.tensor_copy(out=dst, in_=src)
             else:
-                nc.scalar.activation(out=o, in_=src, func=ACT.Copy)
+                nc.scalar.activation(out=dst, in_=src, func=ACT.Copy)
 
-        def turn(n, e, own=False):
-            if e == 0 or own:
-                bank = psum.tile([P, 4, P], F32, name="tp", bufs=2)
-                tb[n, e] = bank
+        def turn_result(n, e, own_bank=False):
+            if e == 0 or own_bank:
+                bank = psum.tile([P, 4, P], F32, name="turned", bufs=2)
+                turned[n, e] = bank
             else:
-                tb[n, e] = tb[n, 0]
-            words = rb[n][:, e, :].bitcast(F32)
-            for k in (0, 1):
-                nc.tensor.transpose(tb[n, e][:, 2 * e + k, :], words[:, P * k : P * (k + 1)], ident[:])
+                turned[n, e] = turned[n, 0]
+            words = rounded[n][:, e, :].bitcast(F32)
+            for u in (0, 1):
+                nc.tensor.transpose(turned[n, e][:, 2 * e + u, :], words[:, P * u : P * (u + 1)], ident[:])
 
-        def turn_copy(n):
-            pg[n] = work.tile([P, 2, 512], BF16, name="pg", align_bytes=64)
-            o = pg[n][:].rearrange("p e x -> p (e x)").bitcast(F32)
+        def copy_turned(n):
+            p_grouped[n] = work.tile([P, 2, F // 2], BF16, name="p_grouped", align_bytes=64)
+            words = p_grouped[n][:].rearrange("p e x -> p (e x)").bitcast(F32)
             nc.scalar.copy(
-                out=o.rearrange("p (e r u) -> p e r u", e=2, u=2),
-                in_=tb[n, 0][:].rearrange("p (e u) r -> p e r u", e=2),
+                out=words.rearrange("p (e r u) -> p e r u", e=2, u=2),
+                in_=turned[n, 0][:].rearrange("p (e u) r -> p e r u", e=2),
             )
 
-        def turn_copy_half(n, e, copy):
+        def copy_turned_half(n, e, copy):
             if e == 0:
-                pg[n] = work.tile([P, 2, 512], BF16, name="pg", align_bytes=64)
+                p_grouped[n] = work.tile([P, 2, F // 2], BF16, name="p_grouped", align_bytes=64)
             copy(
-                out=pg[n][:, e, :].bitcast(F32).rearrange("p (r u) -> p r u", u=2),
-                in_=tb[n, e][:, 2 * e : 2 * e + 2, :].rearrange("p u r -> p r u"),
+                out=p_grouped[n][:, e, :].bitcast(F32).rearrange("p (r u) -> p r u", u=2),
+                in_=turned[n, e][:, 2 * e : 2 * e + 2, :].rearrange("p u r -> p r u"),
             )
 
-        def p_quant(n, parts=1):
-            i, h = pairs[n]
-            codes = work.tile([P, 2 * P], U32, name="pc", align_bytes=64)
+        def quantize_result(n, parts=1):
+            i, h = PAIRS[n]
+            codes = work.tile([P, 2 * P], U32, name="p_codes", align_bytes=64)
+            src = p_grouped[n][:].rearrange("p e x -> p (e x)")
             w = 2 * P // parts
-            src = pg[n][:].rearrange("p e x -> p (e x)")
             for k in range(parts):
                 nc.vector.quantize_mx(
                     out=codes[:, w * k : w * (k + 1)].bitcast(FP8X4),
-                    scales=pscale[:, h, P * i + w * k : P * i + w * (k + 1)],
-                    in_=src[:, 4 * w * k : 4 * w * (k + 1)],
+                    scales=p_scales[:, h, P * i + w * k : P * i + w * (k + 1)],
+                    in_=src[:, PACK * w * k : PACK * w * (k + 1)],
                 )
             nc.sync.dma_start(out=o1[h, :, P * i : P * (i + 2)], in_=codes[:].bitcast(I32))
 
-        def store_scales(lo, hi, engs):
+        def store_scales(first, end, queues):
             for q in range(4):
-                engs[q % len(engs)].dma_start(
-                    out=o2[4 * q : 4 * q + 4, :, 32 * lo : 32 * hi],
-                    in_=pscale[32 * q : 32 * q + 4, :, P * lo : P * hi].bitcast(I32),
+                queues[q % len(queues)].dma_start(
+                    out=o2[4 * q : 4 * q + 4, :, P // 4 * first : P // 4 * end],
+                    in_=p_scales[32 * q : 32 * q + 4, :, P * first : P * end].bitcast(I32),
                 )
 
-        seq = [(n, e) for n in range(8) for e in (0, 1)]
-        state = {"c": 0, "b": 0}
-        done1, done2 = set(), set()
-
-        def pump():
-            while state["c"] < min(16, state["b"] + 2):
-                n, e = seq[state["c"]]
-                i, h = pairs[n][0] + e, pairs[n][1]
-                if i not in done1 or not all([4 * h + q in done2 for q in range(4)]):
-                    return
-                c_mm(n, e)
-                state["c"] += 1
-
-        def q1(i):
-            d1_quant(i)
-            done1.add(i)
-            pump()
-
-        def q2(j):
-            d2_quant(j)
-            done2.add(j)
-            pump()
-
-        def R():
-            r = state["b"]
-            n, e = seq[r]
+        def output_tile(by_vector):
+            r = len(blended)
+            n, e = out_tiles[r]
             blend(n, e)
-            state["b"] += 1
+            blended.append(r)
             pump()
-            last = r == 15
             if r >= 1:
-                tn, tz = seq[r - 1]
-                turn(tn, tz)
-            if e == LC and n >= 1:
-                turn_copy(n - 1)
-            cast(n, e, last)
+                turn_result(*out_tiles[r - 1])
+            if e == 1 and n >= 1:
+                copy_turned(n - 1)
+            round_result(n, e, by_vector or r == len(out_tiles) - 1)
 
-        consumed = 0
         for tok in ORDER:
             arg = [int(v) for v in tok[1:].split(".") if v]
             if tok[0] == "Y":
-                dy_prep(*arg)
-                ready.add((arg[0], arg[1]))
+                t, g, b, e = arg
+                turn_dy(t, g, b, nc.scalar.copy if e else nc.vector.tensor_copy)
+            elif tok[0] == "q":
+                quantize_dy(*arg)
+                quantized_dy.add((arg[0], arg[1], arg[2]))
+            elif tok[0] == "s":
+                activate(CHUNKS[arg[0]], arg[1], sig, ACT.Sigmoid, 1.0)
+            elif tok[0] == "r":
+                activate(CHUNKS[arg[0]], arg[1], slo, ACT.Silu, -1.0)
+            elif tok[0] == "U":
+                silu_by_vector(CHUNKS[arg[0] // 2], arg[0] % 2)
+            elif tok[0] == "S":
+                slope(CHUNKS[arg[0] // 2], arg[0] % 2)
             elif tok[0] == "F":
                 feed(4)
-            elif tok[0] == "A":
-                for fn in FUNCS:
-                    for pair in (0, 1):
-                        if fn[0] == "r":
-                            act(chunks[int(fn[1])], pair, rt, ACT.Silu, -1.0)
-                        else:
-                            act(chunks[int(fn[1])], pair, st, ACT.Sigmoid, 1.0)
-            elif tok[0] == "S":
-                slope_pair(*arg)
             elif tok[0] in "DG":
-                (take2 if arg[0] == 2 else take1)(arg[1], arg[2], tok[0] == "G")
-                consumed += 1
+                unit(arg[0], arg[1], arg[2], tok[0] == "G")
             elif tok[0] == "Q":
-                (q2 if arg[0] == 2 else q1)(arg[1])
-            elif tok[0] == "R":
-                R()
+                quantize_d(*arg)
+                quantized_d.add((arg[0], arg[1]))
+                pump()
+            elif tok[0] in "RV":
+                output_tile(tok[0] == "V")
             elif tok[0] == "P":
-                p_quant(*arg)
+                quantize_result(*arg)
             else:
                 store_scales(0, 4, [nc.sync])
-        turn(7, 1, True)
-        p_quant(6)
-        turn_copy_half(7, 0, nc.scalar.copy)
-        turn_copy_half(7, 1, nc.vector.tensor_copy)
-        p_quant(7, 2)
+
+        turn_result(7, 1, True)
+        quantize_result(6)
+        copy_turned_half(7, 0, nc.scalar.copy)
+        copy_turned_half(7, 1, nc.vector.tensor_copy)
+        quantize_result(7, 2)
         store_scales(4, 8, [nc.sync, nc.scalar])

from contextlib import ExitStack

import concourse.mybir as mybir
from concourse.masks import make_identity

F32 = mybir.dt.float32
BF16 = mybir.dt.bfloat16
U32 = mybir.dt.uint32
I32 = mybir.dt.int32
U8 = mybir.dt.uint8
FP8X4 = mybir.dt.float8_e4m3fn_x4
FP4X4 = mybir.dt.float4_e2m1fn_x4
ACT = mybir.ActivationFunctionType
ALU = mybir.AluOpType

N, O, F = 1024, 512, 1024
P = 128
PACK = 4
GROUP = P * PACK
NB = F // P
FLOPS = 2 * 2 * N * O * F + 2 * N * F * F

SLOPE_FACTOR = {1: -1.0 / (2 * N), 2: -1.0}

CHUNKS = [(0, 0), (1, 0), (0, 1), (1, 1)]

PAIRS = [(0, 0), (2, 0), (0, 1), (2, 1), (4, 0), (4, 1), (6, 0), (6, 1)]

LOADS = "a0 y10 a1 y21 w2 a3 y11 a2 w1".split()

ORDER = """
Y2.0.1.0 s0.1 q2.0.1 s0.0 Y2.0.0.0 U1 s1.1 Y1.0.0.1 Y1.0.1.1 s1.0 U0 Y2.1.1.1 S1 U3 q1.0.1 r3.0 q2.0.0 q1.0.0 S3
F Y2.1.0.1 U2 q2.1.1 Y1.1.0.1 D2.1.1 D2.1.0 r2.1 q2.1.0 S0 S2 q1.1.0 Y1.1.1.1 G2.2.1 D2.0.0 D1.0.0 r2.0 D1.1.0
q1.1.1 G2.2.0 r3.1 D2.0.1 D2.3.0 G1.3.0 D1.3.1 D1.0.1 s3.0 D2.3.1 Q2.0 Q2.3 Q2.2 Q1.3 Q1.0 Q2.1 s2.0 S6 S4
D1.1.1 D2.6.0 G1.2.0 s2.1 S5 G1.4.0 s3.1 D2.4.1 G1.2.1 D2.4.0 D2.6.1 R Q1.1 Q1.2 S7 G2.5.1 G2.7.1 D2.5.0 R R
D2.7.0 Q2.4 Q2.6 Q2.5 Q2.7 G1.7.1 R D1.4.1 G1.7.0 Q1.4 G1.5.0 R G1.6.1 R D1.6.0 D1.5.1 R R P1 Q1.5 P0 R Q1.7 V R
Q1.6 R P2 P3 R P4 V R R X P5
""".split()


def tile_twotaskkroneckergradientcrossfactorema_x2_kernel(
    tc, dy1, w1_words, w1_scales, dy2, w2_words, w2_scales, a, g_old, out_0, out_1, out_2
):
    nc = tc.nc
    dy_rows = {1: dy1, 2: dy2}
    w_bytes = {1: (w1_words, w1_scales), 2: (w2_words, w2_scales)}

    with ExitStack() as ctx:
        keep = ctx.enter_context(tc.tile_pool(name="keep", bufs=1))
        work = ctx.enter_context(tc.tile_pool(name="work", bufs=3))
        psum = ctx.enter_context(tc.psum_pool(name="psum", bufs=2))

        ident = keep.tile([P, P], F32, name="ident")
        make_identity(nc, ident[:])
        warm = keep.tile([P, 2], F32, name="warm")

        ctx.enter_context(tc.manual_schedule())

        dy_raw, dy_codes, dy_scales, w_codes, w_plane = {}, {}, {}, {}, {}
        for t in (1, 2):
            w_codes[t] = keep.tile([P, 2 * F], U8, name="w_codes%d" % t, align_bytes=64)
            w_plane[t] = keep.tile([P, F], U8, name="w_plane%d" % t, align_bytes=64)
            for g in (0, 1):
                dy_raw[t, g] = keep.tile([P, PACK, O], BF16, name="dy_raw%d%d" % (t, g), align_bytes=64)
                dy_codes[t, g] = keep.tile([P, GROUP], U32, name="dy_codes%d%d" % (t, g), align_bytes=64)
                dy_scales[t, g] = keep.tile([P, GROUP], U8, name="dy_scales%d%d" % (t, g), align_bytes=64)
        a_raw, sig, slo = {}, {}, {}
        for c in CHUNKS:
            a_raw[c] = keep.tile([P, PACK, F // 2], BF16, name="a_raw%d%d" % c, align_bytes=64)
            sig[c] = keep.tile([P, PACK * F // 2], F32, name="sig%d%d" % c, align_bytes=64)
            slo[c] = keep.tile([P, PACK * F // 2], F32, name="slo%d%d" % c, align_bytes=64)
        g_rows = {}
        for b in (0, 1):
            g_rows[b] = keep.tile([P, 4, F], BF16, name="g_rows%d" % b, align_bytes=64)
        d2_codes, d2_scales = {}, {}
        for g in (0, 1):
            d2_codes[g] = keep.tile([P, F], U32, name="d2_codes%d" % g, align_bytes=64)
            d2_scales[g] = keep.tile([P, F], U8, name="d2_scales%d" % g, align_bytes=64)
        p_scales = keep.tile([P, 2, F], U8, name="p_scales", align_bytes=64)
        d1_codes = keep.tile([P, NB, 2, P], U32, name="d1_codes", align_bytes=64)
        d1_scales = keep.tile([P, NB, 2, P], U8, name="d1_scales", align_bytes=64)

        nc.vector.memset(w_plane[2][:].bitcast(I32), 0)
        nc.vector.memset(warm[:], 0.0)
        nc.vector.memset(w_plane[1][:].bitcast(I32), 0)

        def load_dy(t, g, parts=1):
            rows = dy_rows[t].rearrange("(g p t) o -> g p t o", p=P, t=PACK)
            n = PACK // parts
            for k in range(0, PACK, n):
                nc.sync.dma_start(out=dy_raw[t, g][:, k : k + n, :], in_=rows[g, :, k : k + n, :])

        def load_a(c):
            g, h = c
            rows = a.rearrange("(g p t) f -> g p t f", p=P, t=PACK)
            nc.sync.dma_start(out=a_raw[c][:], in_=rows[g, :, :, F // 2 * h : F // 2 * (h + 1)])

        def load_w_scales(t, queue):
            for q in range(4):
                queue.dma_start(
                    out=w_plane[t][32 * q : 32 * q + 4, :].bitcast(I32),
                    in_=w_bytes[t][1][0, 4 * q : 4 * q + 4, :].bitcast(I32),
                )

        load_dy(2, 0, 2)
        load_w_scales(2, nc.scalar)
        for tok in LOADS:
            if tok[0] == "y":
                load_dy(int(tok[1]), int(tok[2]))
            elif tok[0] == "a":
                load_a(CHUNKS[int(tok[1])])
            else:
                t = int(tok[1])
                nc.sync.dma_start(out=w_codes[t][:].bitcast(I32), in_=w_bytes[t][0][0].bitcast(I32))
                if t == 1:
                    load_w_scales(1, nc.sync)
        g_view = g_old.rearrange("(b i p) f -> b p i f", p=P, i=4)
        for b in (0, 1):
            nc.sync.dma_start(out=g_rows[b][:], in_=g_view[b])

        nc.scalar.activation(out=warm[:, 1:2], in_=warm[:, 0:1], func=ACT.Sigmoid)

        def tile_of(c, half):
            return slice(PACK * 256 * half, PACK * 256 * (half + 1))

        def by_feature(view):
            return view.rearrange("p (f t) -> p f t", t=PACK)

        def a_by_feature(c, half):
            return a_raw[c][:, :, 256 * half : 256 * (half + 1)].rearrange("p t f -> p f t")

        def activate(c, half, dst, func, scale):
            nc.scalar.activation(
                out=by_feature(dst[c][:, tile_of(c, half)]), in_=a_by_feature(c, half), func=func, scale=scale
            )

        def silu_by_vector(c, half):
            sl = tile_of(c, half)
            nc.vector.scalar_tensor_tensor(
                out=by_feature(slo[c][:, sl]), in0=by_feature(sig[c][:, sl]), scalar=1.0, in1=a_by_feature(c, half),
                op0=ALU.subtract, op1=ALU.mult,
            )

        def slope(c, half):
            sl = tile_of(c, half)
            nc.vector.scalar_tensor_tensor(
                out=slo[c][:, sl], in0=slo[c][:, sl], scalar=1.0, in1=sig[c][:, sl], op0=ALU.subtract, op1=ALU.mult
            )

        dy_grouped = {}

        def turn_dy(t, g, b, copy):
            bank = psum.tile([P, 2, 2, P], F32, name="turned", bufs=2)
            for k in (0, 1):
                words = dy_raw[t, g][:, 2 * b + k, :].bitcast(F32)
                for u in (0, 1):
                    nc.tensor.transpose(bank[:, k, u, :], words[:, u : O // 2 : 2], ident[:])
            grouped = work.tile([P, 2 * P * PACK], BF16, name="dy_grouped", align_bytes=64, bufs=4)
            copy(
                out=grouped[:].bitcast(F32).rearrange("p (t r u) -> p t r u", t=2, u=2),
                in_=bank[:].rearrange("p t u r -> p t r u"),
            )
            dy_grouped[t, g, b] = grouped

        def quantize_dy(t, g, b):
            cols = slice(2 * P * b, 2 * P * (b + 1))
            nc.vector.quantize_mx(
                out=dy_codes[t, g][:, cols].bitcast(FP8X4),
                scales=dy_scales[t, g][:, cols],
                in_=dy_grouped[t, g, b][:],
            )

        units = []
        for tok in ORDER:
            if tok[0] in "DG":
                t, x, y = [int(v) for v in tok[1:].split(".")]
                if t == 2:
                    g, h = CHUNKS[x // 2]
                    units.append((2, g, 4 * h + 2 * (x % 2) + y))
                else:
                    units.append((1, y, x))
        position = {u: k for k, u in enumerate(units)}
        banks = {}
        quantized_dy = set()

        def multiply(k):
            t, g, fb = units[k]
            bank = psum.tile([P, PACK, P], F32, name="unit", bufs=4)
            for q in range(PACK):
                nc.tensor.matmul_mx(
                    out=bank[:, q, :],
                    lhsT=dy_codes[t, g][:, P * q : P * (q + 1)].bitcast(FP8X4),
                    lhsT_scale=dy_scales[t, g][:, P * q : P * (q + 1)],
                    rhs=w_codes[t][:, 2 * P * fb : 2 * P * (fb + 1)].bitcast(FP4X4),
                    rhs_scale=w_plane[t][:, P * fb : P * (fb + 1)],
                    start=True,
                    stop=True,
                )
            banks[k] = bank

        def feed(upto):
            while len(banks) < min(upto, len(units)):
                t, g, fb = units[len(banks)]
                if (t, g, 0) not in quantized_dy or (t, g, 1) not in quantized_dy:
                    return
                multiply(len(banks))

        def apply_slope(k, out, by_gpsimd):
            t, g, fb = units[k]
            slope_part = slo[g, fb // 4][:, PACK * P * (fb % 4) : PACK * P * (fb % 4 + 1)]
            product = banks[k][:].rearrange("p t f -> p f t")
            if by_gpsimd:
                copied = work.tile([P, PACK * P], F32, name="copied", align_bytes=64)
                nc.scalar.activation(out=by_feature(copied[:]), in_=product, func=ACT.Copy, scale=SLOPE_FACTOR[t])
                nc.gpsimd.tensor_tensor(out=out, in0=copied[:], in1=slope_part, op=ALU.mult)
            else:
                nc.vector.scalar_tensor_tensor(
                    out=by_feature(out), in0=by_feature(slope_part), scalar=SLOPE_FACTOR[t], in1=product,
                    op0=ALU.mult, op1=ALU.mult,
                )

        d_grouped = {}

        def unit(t, x, y, by_gpsimd):
            if (t, x) not in d_grouped:
                d_grouped[t, x] = work.tile([P, 2, PACK * P], BF16, name="d_grouped", align_bytes=64, bufs=7)
            k = len(started)
            started.append(k)
            feed(k + 1)
            apply_slope(k, d_grouped[t, x][:, y, :], by_gpsimd)
            feed(k + 5)

        started = []

        def quantize_d(t, x):
            if t == 2:
                g, h = CHUNKS[x // 2]
                first = P * (4 * h + 2 * (x % 2))
                codes, scales = d2_codes[g][:, first : first + 2 * P], d2_scales[g][:, first : first + 2 * P]
            else:
                codes = d1_codes[:, x].rearrange("p g f -> p (g f)")
                scales = d1_scales[:, x].rearrange("p g f -> p (g f)")
            nc.vector.quantize_mx(
                out=codes.bitcast(FP8X4), scales=scales, in_=d_grouped[t, x][:].rearrange("p a b -> p (a b)")
            )

        o0 = out_0.rearrange("(b p) f -> p b f", p=P)
        o1 = out_1.bitcast(I32).rearrange("g p m o -> g p (m o)")
        o2 = out_2.bitcast(I32).rearrange("g r m -> r g m")
        out_tiles = [(n, e) for n in range(NB) for e in (0, 1)]
        products, result, rounded, turned, p_grouped = {}, {}, {}, {}, {}
        blended = []
        quantized_d = set()

        def second_stage(n, e):
            i, h = PAIRS[n][0] + e, PAIRS[n][1]
            bank = psum.tile([P, F // 2], F32, name="product", bufs=2)
            for g in (0, 1):
                nc.tensor.matmul_mx(
                    out=bank[:],
                    lhsT=d1_codes[:, i, g, :].bitcast(FP8X4),
                    lhsT_scale=d1_scales[:, i, g, :],
                    rhs=d2_codes[g][:, F // 2 * h : F // 2 * (h + 1)].bitcast(FP8X4),
                    rhs_scale=d2_scales[g][:, F // 2 * h : F // 2 * (h + 1)],
                    start=(g == 0),
                    stop=(g == 1),
                )
            products[n, e] = bank

        def pump():
            while len(products) < min(len(out_tiles), len(blended) + 2):
                n, e = out_tiles[len(products)]
                i, h = PAIRS[n][0] + e, PAIRS[n][1]
                if (1, i) not in quantized_d or not all([(2, 4 * h + q) in quantized_d for q in range(4)]):
                    return
                second_stage(n, e)

        def blend(n, e):
            i, h = PAIRS[n][0] + e, PAIRS[n][1]
            cols = slice(F // 2 * h, F // 2 * (h + 1))
            if e == 0:
                result[n] = work.tile([P, 2, F // 2], F32, name="result", align_bytes=64)
            nc.vector.scalar_tensor_tensor(
                out=result[n][:, e, :], in0=g_rows[i // 4][:, i % 4, cols], scalar=0.5, in1=products[n, e][:],
                op0=ALU.mult, op1=ALU.add,
            )
            if e == 1:
                nc.sync.dma_start(out=o0[:, i - 1 : i + 1, cols], in_=result[n][:])

        def round_result(n, e, by_vector):
            if e == 0:
                rounded[n] = work.tile([P, 2, F // 2], BF16, name="rounded", align_bytes=64)
            dst = rounded[n][:, e, :].rearrange("q (u p w) -> q u p w", u=2, w=2)
            src = result[n][:, e, :].rearrange("q (p u w) -> q u p w", u=2, w=2)
            if by_vector:
                nc.vector.tensor_copy(out=dst, in_=src)
            else:
                nc.scalar.activation(out=dst, in_=src, func=ACT.Copy)

        def turn_result(n, e, own_bank=False):
            if e == 0 or own_bank:
                bank = psum.tile([P, 4, P], F32, name="turned", bufs=2)
                turned[n, e] = bank
            else:
                turned[n, e] = turned[n, 0]
            words = rounded[n][:, e, :].bitcast(F32)
            for u in (0, 1):
                nc.tensor.transpose(turned[n, e][:, 2 * e + u, :], words[:, P * u : P * (u + 1)], ident[:])

        def copy_turned(n):
            p_grouped[n] = work.tile([P, 2, F // 2], BF16, name="p_grouped", align_bytes=64)
            words = p_grouped[n][:].rearrange("p e x -> p (e x)").bitcast(F32)
            nc.scalar.copy(
                out=words.rearrange("p (e r u) -> p e r u", e=2, u=2),
                in_=turned[n, 0][:].rearrange("p (e u) r -> p e r u", e=2),
            )

        def copy_turned_half(n, e, copy):
            if e == 0:
                p_grouped[n] = work.tile([P, 2, F // 2], BF16, name="p_grouped", align_bytes=64)
            copy(
                out=p_grouped[n][:, e, :].bitcast(F32).rearrange("p (r u) -> p r u", u=2),
                in_=turned[n, e][:, 2 * e : 2 * e + 2, :].rearrange("p u r -> p r u"),
            )

        def quantize_result(n, parts=1):
            i, h = PAIRS[n]
            codes = work.tile([P, 2 * P], U32, name="p_codes", align_bytes=64)
            src = p_grouped[n][:].rearrange("p e x -> p (e x)")
            w = 2 * P // parts
            for k in range(parts):
                nc.vector.quantize_mx(
                    out=codes[:, w * k : w * (k + 1)].bitcast(FP8X4),
                    scales=p_scales[:, h, P * i + w * k : P * i + w * (k + 1)],
                    in_=src[:, PACK * w * k : PACK * w * (k + 1)],
                )
            nc.sync.dma_start(out=o1[h, :, P * i : P * (i + 2)], in_=codes[:].bitcast(I32))

        def store_scales(first, end, queues):
            for q in range(4):
                queues[q % len(queues)].dma_start(
                    out=o2[4 * q : 4 * q + 4, :, P // 4 * first : P // 4 * end],
                    in_=p_scales[32 * q : 32 * q + 4, :, P * first : P * end].bitcast(I32),
                )

        def output_tile(by_vector):
            r = len(blended)
            n, e = out_tiles[r]
            blend(n, e)
            blended.append(r)
            pump()
            if r >= 1:
                turn_result(*out_tiles[r - 1])
            if e == 1 and n >= 1:
                copy_turned(n - 1)
            round_result(n, e, by_vector or r == len(out_tiles) - 1)

        for tok in ORDER:
            arg = [int(v) for v in tok[1:].split(".") if v]
            if tok[0] == "Y":
                t, g, b, e = arg
                turn_dy(t, g, b, nc.scalar.copy if e else nc.vector.tensor_copy)
            elif tok[0] == "q":
                quantize_dy(*arg)
                quantized_dy.add((arg[0], arg[1], arg[2]))
            elif tok[0] == "s":
                activate(CHUNKS[arg[0]], arg[1], sig, ACT.Sigmoid, 1.0)
            elif tok[0] == "r":
                activate(CHUNKS[arg[0]], arg[1], slo, ACT.Silu, -1.0)
            elif tok[0] == "U":
                silu_by_vector(CHUNKS[arg[0] // 2], arg[0] % 2)
            elif tok[0] == "S":
                slope(CHUNKS[arg[0] // 2], arg[0] % 2)
            elif tok[0] == "F":
                feed(4)
            elif tok[0] in "DG":
                unit(arg[0], arg[1], arg[2], tok[0] == "G")
            elif tok[0] == "Q":
                quantize_d(*arg)
                quantized_d.add((arg[0], arg[1]))
                pump()
            elif tok[0] in "RV":
                output_tile(tok[0] == "V")
            elif tok[0] == "P":
                quantize_result(*arg)
            else:
                store_scales(0, 4, [nc.sync])

        turn_result(7, 1, True)
        quantize_result(6)
        copy_turned_half(7, 0, nc.scalar.copy)
        copy_turned_half(7, 1, nc.vector.tensor_copy)
        quantize_result(7, 2)
        store_scales(4, 8, [nc.sync, nc.scalar])
